import numpy as np, ml_dtypes
CORES = [2,6,10,14,18,22,26,30]
N = 8
BF = ml_dtypes.bfloat16
def gentries(a):
    return np.ascontiguousarray(a.reshape(8, 16, -1).transpose(0, 2, 1)).reshape(8, -1)
def gtable(e):
    e = np.asarray(e); return np.ascontiguousarray(e.reshape(8, -1, 16).transpose(0, 2, 1)).reshape(128, -1).astype(np.int32)
S, A, DB, RO, MX = 4096, 2, 5, 2, 7
U = 128 >> DB
def parts(rng):
    nx = rng.integers(0, S, (N, 8, A, S))
    nx[:, 1::3] = (np.arange(S) + rng.integers(1, S // 8, nx[:, 1::3].shape)) % S
    lev = rng.random((N, 8, 16, 1), dtype=np.float32) * np.float32(0.75) + np.float32(0.25)
    rw = np.minimum(np.floor(rng.random((N, 8, 16, A * S), dtype=np.float32) * lev * np.float32(MX + 1)), np.float32(MX))
    cap = rng.integers(MX + 1, 129, (N, 8, 16, 1)); act = rng.integers(0, A, (N, 8, S))
    return nx, rw, cap, act
def pack(nx, rw, cap, act):
    return {"nx": np.stack([gtable(a.reshape(8, -1)) for a in nx]), "rw": np.ascontiguousarray(rw).reshape(N, 128, A * S).astype(np.float32).astype(BF),
            "cap": np.ascontiguousarray(cap).reshape(N, 128, 1).astype(np.float32), "act0": np.stack([gtable(a) for a in act])}
def stage(rng, nx, rw, cap, g, to, rew):
    cap[:, g] = 128
    for p in range(N):
        z, e, f = [int(v) for v in rng.permutation(S)[:3]]
        nx[p, g] = np.array([z, e, f])[to[p]]
        nx[p, g, :, z] = z; nx[p, g, :, e] = f; nx[p, g, :, f] = f
        rew[p, :, :, z] = 0; rew[p, :, :, e] = 0; rew[p, :, :, f] = U
    rw[:, g] = rew.reshape(N, 16, A * S)
def swing(rng):
    to = np.where(rng.random(S) < 0.4, 2 * rng.integers(0, 2, (1, A, S)), rng.integers(0, 3, (N, A, S)))
    rew = rng.integers(0, MX + 1, (N, 16, A, S)) * (rng.random(S) < 0.5)
    return to, rew
def brim(rng):
    to = 1 + (rng.random((N, A, S)) < 0.3).astype(np.int64)
    short = rng.random((N, 16, A, S)) * (16 * N) < 1
    return to, np.where(short, U - 1, rng.integers(U, MX + 1, short.shape))
def tug(rng):
    h = N // 2; o = rng.permutation(N); p, q = o[:h], o[h:2 * h]
    low = rng.integers(0, U + 1, (h, 16, A, S)) * (rng.random(S) < 0.7)
    high = U - low.reshape(16 * h, A, S)[rng.permutation(16 * h)].reshape(low.shape)
    b = rng.random((h, A, S)) < 0.5
    to = np.zeros((N, A, S), np.int64); rew = np.zeros((N, 16, A, S), np.int64)
    to[p] = np.where(b, 1, 0); to[q] = np.where(b, 0, 1)
    rew[p] = np.where(b[:, None], high, low); rew[q] = np.where(b[:, None], low, high)
    x = rng.random(rew.shape) * (16 * N)
    rew = rew + (x < 0.5).astype(np.int64) - (x > 16 * N - 0.5).astype(np.int64)
    return to, np.minimum(np.maximum(rew, 0), MX)
def setup_inputs(rng):
    return pack(*parts(rng))
def setup_inputs_ties(rng):
    nx, rw, cap, act = parts(rng); w = rw.reshape(N, 8, 16, A, S)
    nx[:, 0::4, 1:] = nx[:, 0::4, :1]; w[:, 0::4, :, 1:] = w[:, 0::4, :, :1]
    for g in (1, 5):
        m = rng.random(S) < 0.5
        nx[:, g] = np.where(m, nx[:, g, :1], nx[:, g]); w[:, g] = np.where(m, w[:, g, :, :1], w[:, g])
    for g in (2, 6):
        nx[:, g, 1:] = nx[:, g, :1]; cap[:, g] = 128
        w[:, g] = (4 * (rng.random((N, 16, 1, S)) < 0.3)).astype(np.float32)
        q = int(rng.integers(0, N)); i = int(rng.integers(0, 16))
        w[q, g, i] = 1; w[q, g, i, A - 1] = rng.integers(0, 3, S)
    for g in (3, 7):
        w[:, g] = MX * (rng.random((N, 16, A, S)) < 0.3).astype(np.float32); cap[:, g] = MX + 1
    return pack(nx, w, cap, act)
def setup_inputs_full(rng):
    nx, rw, cap, act = parts(rng)
    v = rng.integers(1, MX + 1, (N, 8, 16, 1))
    rw = np.where(rng.random(rw.shape, dtype=np.float32) < 0.03, rw, v.astype(np.float32))
    near = v * 2 ** DB + rng.integers(-1, 2, v.shape); ends = rng.choice(np.array([MX + 1, MX + 2, 127, 128]), v.shape)
    cap = np.minimum(np.maximum(np.where(rng.random(v.shape) < 0.6, near, ends), MX + 1), 128)
    rw[:, 0] = MX; rw[:, 1] = np.where(rng.random(rw[:, 1].shape) < 0.01, 1 + rng.integers(0, MX, rw[:, 1].shape), 0)
    return pack(nx, rw, cap, act)
def setup_inputs_chains(rng):
    nx, rw, cap, act = parts(rng); s = np.arange(S); a = np.arange(A)[:, None]
    nx[:, 0] = s; nx[:, 1] = np.minimum(s + 1 + a, S - 1); nx[:, 2] = (s - 1 - a) % S
    nx[:, 3] = rng.integers(0, S, (N, A, 1)); nx[:, 4] = np.argsort(rng.random((N, A, S)), axis=-1)
    nx[:, 5] = (S - 1) * rng.integers(0, 2, (N, A, S)); nx[:, 6, ::2] = s ^ 1; nx[:, 7] = nx[:1, 7]
    act[:, 1] = 0; act[:, 2] = A - 1; act[:, 4] = act[:1, 4]
    return pack(nx, rw, cap, act)
def setup_inputs_loud(rng):
    nx, rw, cap, act = parts(rng); o = rng.permutation(N); big = np.zeros((N, 8, 1, 1), bool)
    for g in range(8): big[o[g % N], g] = True
    big[:, 2] = True
    rw = np.where(big | (rng.random(rw.shape, dtype=np.float32) < 0.01), rw, np.float32(0))
    rw[o[0], 2] = 0; rw[:, 3] = 0
    for p in range(N):
        if not big[p, 7, 0, 0]: rw[p, 7] = 0
    for g, make in ((1, swing), (5, brim), (6, tug)):
        to, rew = make(rng); stage(rng, nx, rw, cap, g, to, rew)
    return pack(nx, rw, cap, act)
def setup_inputs_spread(rng):
    nx, rw, cap, act = parts(rng)
    e = np.exp2(rng.integers(-2, 3, (N, 8, 16, 1)) + rng.integers(-2, 3, (N, 8, 1, A * S))).astype(np.float32)
    rw = np.minimum(np.floor(np.float32(MX + 1) * rng.random(rw.shape, dtype=np.float32) ** e), np.float32(MX))
    nx = np.minimum(np.floor(S * rng.random(nx.shape) ** np.exp2(rng.integers(-2, 3, (N, 8, 1, 1)))).astype(np.int64), S - 1)
    cap = np.minimum(np.floor((MX + 1) * np.exp2(rng.random(cap.shape) * np.log2(128 / (MX + 1)) * 1.02)).astype(np.int64), 128)
    act = np.minimum(np.floor(A * rng.random(act.shape) ** 3).astype(np.int64), A - 1)
    return pack(nx, rw, cap, act)
def check_inputs(d):
    bad = []
    for k, lo, hi in (("nx", 0, S - 1), ("rw", 0, MX), ("cap", MX + 1, 128), ("act0", 0, A - 1)):
        v = np.asarray(d[k]).astype(np.float32)
        if not np.all((v >= lo) & (v <= hi) & (v == np.floor(v))): bad.append("range of " + k)
    return bad
def reference(nx, rw, cap, act0):
    n = np.stack([gentries(a) for a in nx]).astype(np.int64).reshape(N, 8, A, S)
    w = rw.astype(np.float32).astype(np.int32).reshape(N, 8, 16, A, S); c = cap.astype(np.int32).reshape(N, 8, 16, 1)
    act = np.stack([gentries(a) for a in act0]).astype(np.int64)
    for rnd in range(RO):
        t = np.take_along_axis(n, act[:, :, None, :], 2)[:, :, 0]
        r = np.take_along_axis(w, act[:, :, None, None, :], 3)[:, :, :, 0]
        for k in range(DB):
            r = np.minimum(r + np.take_along_axis(r, t[:, :, None, :], 3), c)
            t = np.take_along_axis(t, t, 2)
        q = np.zeros((8, A, S), np.int64)
        for p in range(N):
            for a in range(A):
                v = w[p][:, :, a] + np.take_along_axis(r[p], n[p][:, a][:, None, :], 2)
                q[:, a] += np.add.reduce(np.minimum(v, c[p]), axis=1)
        best = np.argmax(q, axis=1)
        act = np.stack([best for p in range(N)])
    return {"yr": r.reshape(N, 128, S).astype(np.float32).astype(BF), "ya": np.stack([gtable(a) for a in act]).astype(np.float32)}

from concourse.bass import DstId, RemoteDMATransfer
from concourse.mybir import AluOpType, ActivationFunctionType

S = 4096
CH = 1024
MA = 128
SS = 768
BF, F32, I32, U16, F16 = "bfloat16", "float32", "int32", "uint16", "float16"

SCRATCH = {
    "rwb": ("sbuf", [128, 2 * S], BF),
    "y0": ("sbuf", [128, S], BF), "y1": ("sbuf", [128, S], BF), "yc": ("sbuf", [128, S], BF),
    "w0": ("sbuf", [128, S], BF), "w1": ("sbuf", [128, S], BF), "w2": ("sbuf", [128, S], BF),
    "m0": ("sbuf", [128, S], BF), "m1": ("sbuf", [128, S], BF),
    "tmp": ("sbuf", [128, 2048], BF),
    "land0": ("sbuf", [128, 2048], F16), "land1": ("sbuf", [128, 2048], F16),
    "nxi": ("sbuf", [128, 512], I32), "acti": ("sbuf", [128, 256], I32),
    "capf": ("sbuf", [128, 4], F32), "capd": ("sbuf", [128, 4], F32), "capb": ("sbuf", [128, 8], BF),
    "a1": ("sbuf", [128, 512], I32), "a2": ("sbuf", [128, 512], I32),
    "dl1": ("sbuf", [128, 256], F32), "dl2": ("sbuf", [128, 256], F32),
    "d1": ("sbuf", [128, 256], BF), "d2": ("sbuf", [128, 256], BF),
    "orf": ("sbuf", [128, 256], F32), "sloc": ("sbuf", [128, 256], F32), "i16": ("sbuf", [128, 256], F32),
    "pci": ("sbuf", [128, 4], I32), "pmi": ("sbuf", [128, 4], I32), "pmf": ("sbuf", [128, 4], F32),
    "orw": ("sbuf", [128, 256], U16), "op0": ("sbuf", [128, 256], U16), "nq": ("sbuf", [128, 512], U16),
    "o0": ("sbuf", [128, 256], U16), "o1": ("sbuf", [128, 256], U16), "o2": ("sbuf", [128, 256], U16),
    "o3": ("sbuf", [128, 256], U16), "o4": ("sbuf", [128, 256], U16),
    "ones": ("sbuf", [128, 144], BF), "za": ("sbuf", [128, 144], BF), "zb": ("sbuf", [128, 144], BF),
    "zp": ("sbuf", [128, 144], BF), "zn": ("sbuf", [128, 144], BF),
    "idp": ("sbuf", [128, 128], BF), "idn": ("sbuf", [128, 128], BF), "id16": ("sbuf", [128, 128], BF),
    "id256": ("sbuf", [128, 128], BF), "idh": ("sbuf", [128, 128], F16),
    "cw": ("sbuf", [128, 256], BF), "yab": ("sbuf", [128, 256], F32),
    "px0": ("psum", [128, 512], F32), "px1": ("psum", [128, 512], F32), "pa": ("psum", [128, 2048], F32),
    "ps0": ("psum", [128, 512], F32), "ps1": ("psum", [128, 512], F32),
}
PSUM = ("px0", "px1", "pa", "ps0", "ps1")
SEMAPHORES = (["cv", "cs", "ct", "cg", "l_act", "l_nx", "l_cap", "l_rw0", "l_rw1", "l_rw2", "l_rw3",
               "wa0", "wb0", "wa1", "wb1", "sent", "issued", "s_yr", "s_ya", "yc0", "yc1", "yc2", "yc3"]
              + ["arr%d%d%d" % (r, p, w) for r in range(2) for p in range(2) for w in range(8)])


def rank_program(g, core, T, topo):
    rank = T.rank_of(core)
    if rank is None:
        return
    ALU, ACT = AluOpType, ActivationFunctionType
    Q = {"v": g.vector, "s": g.scalar, "t": g.tensor, "y": g.sync, "g": g}
    total = {}
    waited = {}
    known = {q: {} for q in Q}
    clock = {}
    hist = {}

    def A(name, lo, hi, step=1):
        ap = T[name][:, lo:hi] if step == 1 else T[name][:, lo:hi:step]
        return (ap, name, lo, hi)

    def need(q, ev):
        sem, val = ev
        if known[q].get(sem, 0) >= val:
            return
        Q[q].wait_ge(T.sem[sem], val)
        waited[sem] = max(waited.get(sem, 0), val)
        known[q][sem] = val
        for s2, v2 in clock.get(ev, {}).items():
            if known[q].get(s2, 0) < v2:
                known[q][s2] = v2

    def deps(q, reads, writes):
        want = {}
        for views, wr in ((reads, False), (writes, True)):
            for _, name, lo, hi in views:
                for q2, ev, lo2, hi2, wr2 in hist.get(name, []):
                    if name in PSUM and q2 != q:
                        hit = lo // 512 <= (hi2 - 1) // 512 and lo2 // 512 <= (hi - 1) // 512
                    elif q == "t" and q2 == "t":
                        hit = False
                    else:
                        hit = (wr or wr2) and lo < hi2 and lo2 < hi
                    if hit and want.get(ev[0], 0) < ev[1]:
                        want[ev[0]] = ev[1]
        for sem in sorted(want, key=lambda s: (s == "c" + q, s)):
            need(q, (sem, want[sem]))

    def record(q, ev, reads, writes, seen):
        ck = dict(clock.get(ev, {}))
        for s2, v2 in seen.items():
            if ck.get(s2, 0) < v2:
                ck[s2] = v2
        clock[ev] = ck
        for views, wr in ((reads, False), (writes, True)):
            for _, name, lo, hi in views:
                hist.setdefault(name, []).append((q, ev, lo, hi, wr))

    def op(q, make, reads, writes):
        deps(q, reads, writes)
        sem = "c" + q
        total[sem] = total.get(sem, 0) + 1
        make().then_inc(T.sem[sem], 1)
        record(q, (sem, total[sem]), reads, writes, known[q])

    def dma(q, out, in_, sem, val, reads, writes):
        deps(q, reads, writes)
        total[sem] = total.get(sem, 0) + 16
        Q[q].dma_start(out, in_).then_inc(T.sem[sem], 16)
        record("dma", (sem, val), reads, writes, known[q])

    def mm(items, signal=True):
        reads = [x for it in items for x in it[1:3]]
        writes = [it[0] for it in items]
        deps("t", reads, writes)
        ins = None
        for o, l, r, st, sp in items:
            ins = g.tensor.matmul(o[0], l[0], r[0], st, sp)
        val = total.get("ct", 0) + 1
        if signal:
            total["ct"] = val
            ins.then_inc(T.sem["ct"], 1)
        record("t", ("ct", val), reads, writes, known["t"])

    def ind(win, off):
        return win[0].indirect(off[0])

    def ts(out, in0, s1, s2, op0, op1=None, off=None):
        reads = [in0] + [s for s in (s1, s2) if isinstance(s, tuple)] + ([off] if off else [])
        a1 = s1[0] if isinstance(s1, tuple) else s1
        a2 = s2[0] if isinstance(s2, tuple) else s2
        src = ind(in0, off) if off else in0[0]
        if op1 is None:
            op("v", lambda: g.vector.tensor_scalar(out[0], src, a1, None, op0), reads, [out])
        else:
            op("v", lambda: g.vector.tensor_scalar(out[0], src, a1, a2, op0, op1), reads, [out])

    def tt(out, in0, in1, alu, off=None):
        src = ind(in0, off) if off else in0[0]
        op("v", lambda: g.vector.tensor_tensor(out[0], src, in1[0], alu),
           [in0, in1] + ([off] if off else []), [out])

    def cp(out, in_):
        op("v", lambda: g.vector.tensor_copy(out[0], in_[0]), [in_], [out])

    def act(out, in_, func, bias=None, scale=None, off=None):
        kw = {}
        reads = [in_] + ([off] if off else [])
        if bias is not None:
            kw["bias"] = bias[0]
            reads.append(bias)
        if scale is not None:
            kw["scale"] = scale
        src = ind(in_, off) if off else in_[0]
        op("s", lambda: g.scalar.activation(out[0], src, func, **kw), reads, [out])

    def wv(a, s0, s1):
        base = (s0 // CH) * CH + a * CH
        return A("rwb", base + s0, base + s1)

    def fold(dst, src, z, start, stop):
        name, lo, hi = src[1:]
        mm([(dst, A(z, 15 - i, 143 - i), A(name, lo + i, hi, 16), start and i == 0, stop and i == 15)
            for i in range(16)])

    capf, capd, capb = A("capf", 0, 1), A("capd", 0, 1), A("capb", 0, 1)
    idp, idn, id16, id256, idh = [A(x, 0, 128) for x in ("idp", "idn", "id16", "id256", "idh")]

    dma("y", T.acti[:], T.act0[:], "l_act", 16, [], [A("acti", 0, 256)])
    dma("s", T.nxi[:], T.nx[:], "l_nx", 16, [], [A("nxi", 0, 512)])
    dma("y", capf[0], T.cap[:], "l_cap", 16, [], [A("capf", 0, 4)])
    for c in range(4):
        for a, q in ((0, "y"), (1, "s")):
            w = wv(a, c * CH, (c + 1) * CH)
            dma(q, w[0], T.rw[:, a * S + c * CH:a * S + (c + 1) * CH], "l_rw%d" % c, 32, [], [w])

    op("g", lambda: g.iota(T.pci[:, 0:1], [[0, 1]], 0, 1), [], [A("pci", 0, 1)])
    op("g", lambda: g.iota(T.i16[:], [[0, 4], [16, 64]], 0, 0, allow_small_or_imprecise_dtypes=True),
       [], [A("i16", 0, 256)])
    op("g", lambda: g.iota(T.ones[:], [[0, 144]], 1, 0, allow_small_or_imprecise_dtypes=True),
       [], [A("ones", 0, 144)])
    op("g", lambda: g.affine_select(T.idp[:], T.ones[:, 0:128], [[-1, 128]], ALU.is_equal, 0.0, 0, 1),
       [A("ones", 0, 128)], [idp])
    op("g", lambda: g.affine_select(T.za[:], T.ones[:], [[0, 9], [1, 16]], ALU.is_equal, 0.0, -15, 0),
       [A("ones", 0, 144)], [A("za", 0, 144)])
    op("g", lambda: g.affine_select(T.zb[:], T.za[:], [[-16, 9], [0, 16]], ALU.is_ge, 0.0, 0, 1),
       [A("za", 0, 144)], [A("zb", 0, 144)])
    op("g", lambda: g.affine_select(T.zp[:], T.zb[:], [[16, 9], [0, 16]], ALU.is_ge, 0.0, 15, -1),
       [A("zb", 0, 144)], [A("zp", 0, 144)])
    op("v", lambda: g.vector.memset(T.w0[:], 0.0), [], [A("w0", 0, S)])
    ts(A("pmi", 0, 1), A("pci", 0, 1), 15, None, ALU.bitwise_and)
    cp(A("pmf", 0, 1), A("pmi", 0, 1))
    ts(A("sloc", 0, 256), A("i16", 0, 256), A("pmf", 0, 1), 1.0 / CH, ALU.add, ALU.mult)
    act(id16, idp, ACT.Copy, scale=1.0 / 16)
    act(id256, idp, ACT.Copy, scale=256.0)
    act(idn, idp, ACT.Copy, scale=-1.0)
    act(A("zn", 0, 144), A("zp", 0, 144), ACT.Copy, scale=-1.0)

    def r_offsets(m0, m1, av):
        tt(A("orf", m0, m1), av, A("sloc", m0, m1), ALU.add)
        ts(A("orw", m0, m1), A("orf", m0, m1), float(CH), None, ALU.mult)

    def digits(m0, m1, av, t1, t2):
        tt(t1, av, A("dl1", m0, m1), ALU.mult)
        tt(t2, av, A("dl2", m0, m1), ALU.mult)
        tt(A("d1", m0, m1), t1, A("a1", m0, m1), ALU.add)
        tt(A("d2", m0, m1), t2, A("a2", m0, m1), ALU.add)

    def lists_mm(m0, m1, px):
        w = m1 - m0
        x1, x2 = A("d1", m0, m1), A("d2", m0, m1)
        mm([(A(px, 0, w), idp, x1, True, False), (A(px, 0, w), idp, x2, False, True),
            (A(px, w, 2 * w), id16, x1, True, False), (A(px, w, 2 * w), id256, x2, False, True)])

    def lists_cp(m0, m1, px):
        w = m1 - m0
        cp(A("op0", m0, m1), A(px, w, 2 * w))
        cp(A("o0", m0, m1), A(px, 0, w))

    def w0_dma(r):
        dma("y", T.w0[0::16, :], T.d1[:], "wa%d" % r, 16, [A("d1", 0, 256)], [A("w0", 0, S)])
        first = hist["w0"].pop()
        dma("y", T.w0[1::16, :], T.d2[:], "wb%d" % r, 16, [A("d2", 0, 256)], [A("w0", 0, S)])
        hist["w0"].append(first)

    def rinit(q, s0, s1):
        c = s0 // CH
        win, off, out = A("rwb", 2 * CH * c, 2 * CH * (c + 1)), A("orw", s0 // 16, s1 // 16), A("y0", s0, s1)
        if q == "v":
            ts(out, win, -1.0, capd, ALU.mult, ALU.add, off=off)
        else:
            act(out, win, ACT.Identity, bias=capd, scale=-1.0, off=off)

    def ystep(k, s0, s1):
        src, dst = "y%d" % ((k - 1) % 2), "y%d" % (k % 2)
        tt(A(dst, s0, s1), A(src, 0, S), A("yc", s0, s1), ALU.add, off=A("o%d" % (k - 1), s0 // 16, s1 // 16))

    def ycopy(k, s0, s1):
        sem, src = "yc%d" % (s0 // CH), A("y%d" % (k % 2), s0, s1)
        dma("y", T.yc[:, s0:s1], src[0], sem, total.get(sem, 0) + 16, [src], [A("yc", s0, s1)])

    def ypiece(k, j):
        ystep(k, CH * j, CH * (j + 1))
        if k < 4 or j > 0:
            ycopy(k, 2560 if (k, j) == (4, 2) else CH * j, CH * (j + 1))

    def tstep(k, h):
        src = "w0" if k == 1 else "w%d" % (1 + k % 2)
        dst = A("w%d" % (1 + (k - 1) % 2), 2048 * h, 2048 * (h + 1))
        off = A("op0" if k == 1 else "o%d" % (k - 1), 128 * h, 128 * (h + 1))
        act(dst, A(src, 0, S), ACT.Copy, off=off)
        fold(A("px%d" % h, 0, 128), dst, "zp", True, True)

    def conv(k, h):
        cp(A("o%d" % k, 128 * h, 128 * (h + 1)), A("px%d" % h, 0, 128))

    def doublings(mid1, extra):
        for k in range(1, 5):
            ypiece(k, 0)
            ypiece(k, 1)
            tstep(k, 0)
            if k == 1:
                mid1()
            else:
                conv(k - 1, 1)
            ypiece(k, 2)
            ypiece(k, 3)
            tstep(k, 1)
            conv(k, 0)
            extra(k)
        parts = [(0, 512), (512, 1024), (2048, 2560)]
        bank = [A("pa", 512 * j, 512 * (j + 1)) for j in range(3)]
        tm = [A("tmp", 512 * j, 512 * (j + 1)) for j in range(3)]
        act(A("tmp", 0, 1024), A("y0", 0, S), ACT.Copy, off=A("o4", 0, 64))
        ystep(5, 1024, 2048)
        mm([(bank[j], idp, A("y0", parts[j][0], parts[j][1]), True, False) for j in range(3)])
        mm([(bank[0], idp, tm[0], False, True)])
        mm([(bank[1], idp, tm[1], False, True)])
        conv(4, 1)
        ystep(5, 2560, S)
        act(A("y1", 0, 512), bank[0], ACT.Copy)
        act(tm[2], A("y0", 0, S), ACT.Copy, off=A("o4", 128, 160))
        mm([(bank[2], idp, tm[2], False, True)])
        act(A("y1", 512, 1024), bank[1], ACT.Copy)
        act(A("y1", 2048, 2560), bank[2], ACT.Copy)

    n = len(T.cores)

    def far_of(who):
        c0 = T.cores[who]
        return [who ^ d for d in range(1, n) if topo.chip(T.cores[who ^ d]) != topo.chip(c0)]

    far = far_of(rank)
    near = [p for p in range(n) if p != rank and p not in far]
    far_mask = topo.mask(core, T.cores[far[0]])
    near_mask = topo.mask(core, T.cores[near[0]]) & ~far_mask
    n_far, n_near = bin(far_mask).count("1"), bin(near_mask).count("1")
    senders = near + sorted(far, key=lambda p: far_of(p).index(rank))

    def slot(r, part, who):
        lo = (part * n + who) * MA
        return A("land%d" % r, lo, lo + MA)

    def send(r, part):
        mine = slot(r, part, rank)
        cp(mine, A("px%d" % part, 0, MA))
        deps("g", [mine], [])
        tr = []
        for group, mask in ((far, far_mask), (near, near_mask)):
            ids = [DstId(rid=topo.addr(T.cores[p])[0], pnc=topo.addr(T.cores[p])[1]) for p in group]
            tr.append(RemoteDMATransfer(dst_ids=ids, dma_engine_mask=mask,
                                        remote_sem=T.sem["arr%d%d%d" % (r, part, rank)],
                                        srcs=[mine[0]], dsts=[mine[0] for _ in group]))
        g.remote_dma_fused(tr, local_sem=T.sem["sent"])
        total["sent"] = total.get("sent", 0) + n_far + n_near
        for p in senders:
            sem = "arr%d%d%d" % (r, part, p)
            total[sem] = n_near if p in near else n_far
            record("net", (sem, total[sem]), [], [slot(r, part, p)], {})

    def summed(r, part):
        out = A("ps%d" % part, 0, MA)
        for j, who in enumerate([rank] + senders):
            mm([(out, idh, slot(r, part, who), j == 0, j == n - 1)], j == n - 1)
        return out

    def qv(a, s0, s1):
        tt(A("m%d" % a, s0, s1), A("y1", 0, S), wv(a, s0, s1), ALU.max,
           off=A("nq", 256 * a + s0 // 16, 256 * a + s1 // 16))

    def values(r):
        cuts = ((0, 512), (512, SS))

        def pre(a, s0, which=(0, 1)):
            return [(A("pa", CH * a + cuts[j][0], CH * a + cuts[j][1]), idn,
                     wv(a, s0 + cuts[j][0], s0 + cuts[j][1]), True, False) for j in which]

        def qs(a, s0):
            act(A("tmp", CH * a, CH * a + SS), A("y1", 0, S), ACT.Copy,
                off=A("nq", 256 * a + s0 // 16, 256 * a + (s0 + SS) // 16))

        def add(a):
            mm([(A("pa", CH * a + lo, CH * a + hi), idp, A("tmp", CH * a + lo, CH * a + hi), False, True)
                for lo, hi in cuts])

        def relu(a, s0):
            act(A("m%d" % a, s0, s0 + SS), A("pa", CH * a, CH * a + SS), ACT.Relu)

        def fo(a, c, stop=False):
            fold(A("px%d" % (c // 2), 64 * (c % 2), 64 * (c % 2 + 1)), A("m%d" % a, CH * c, CH * (c + 1)),
                 ("zp", "zn")[a], False, stop)

        mm(pre(1, 0, (1,)) + [(A("px%d" % h, 0, MA), idp, A("cw", MA * h, MA * (h + 1)), True, False) for h in (0, 1)])
        mm(pre(0, 0) + pre(1, 0, (0,)))
        qs(0, 0)
        qv(0, CH, 2 * CH)
        add(0)
        fo(0, 1)
        qv(0, SS, CH)
        qs(1, 0)
        qv(1, CH, 2 * CH)
        add(1)
        relu(0, 0)
        fo(0, 0)
        fo(1, 1)
        qv(1, SS, CH)
        relu(1, 0)
        fo(1, 0, True)
        mm(pre(0, 2 * CH))
        qs(0, 2 * CH)
        add(0)
        mm(pre(1, 2 * CH))
        qv(0, 3 * CH, 3 * CH + 512)
        send(r, 0)
        qv(0, 3 * CH + 512, S)
        fo(0, 3)
        qs(1, 2 * CH)
        add(1)
        qv(0, 2 * CH + SS, 3 * CH)
        qv(1, 3 * CH, S)
        relu(0, 2 * CH)
        fo(0, 2)
        fo(1, 3)
        qv(1, 2 * CH + SS, 3 * CH)
        relu(1, 2 * CH)
        fo(1, 2, True)
        send(r, 1)

    av = A("ps0", 0, 256)
    cp(av, A("acti", 0, 256))
    ts(capd, capf, 1.0 / 32, None, ALU.mult)
    r_offsets(0, 256, av)
    rinit("s", 0, 1024)
    ts(A("a1", 0, 512), A("nxi", 0, 512), S - 16, None, ALU.bitwise_and)
    ts(A("a2", 0, 512), A("nxi", 0, 512), 15, None, ALU.bitwise_and)
    tt(A("dl1", 0, 256), A("a1", 256, 512), A("a1", 0, 256), ALU.subtract)
    tt(A("dl2", 0, 256), A("a2", 256, 512), A("a2", 0, 256), ALU.subtract)
    digits(0, 256, av, A("ps0", 256, 512), A("ps1", 0, 256))
    w0_dma(0)
    lists_mm(0, 256, "px0")
    rinit("s", 1024, 2048)
    lists_cp(0, 256, "px0")
    cp(A("yc", 0, 1024), A("y0", 0, 1024))
    cp(A("yc", 1024, 2048), A("y0", 1024, 2048))
    rinit("s", 2048, 2560)
    rinit("v", 2560, 3072)
    ycopy(0, 2048, 3072)
    rinit("s", 3072, 3584)
    rinit("v", 3584, S)
    ycopy(0, 3072, S)
    for c in range(4):
        fold(A("pa", 64 * c, 64 * c + 64), wv(1, CH * c, CH * c + CH), "zp", True, False)
        fold(A("pa", 64 * c, 64 * c + 64), wv(0, CH * c, CH * c + CH), "zn", False, True)

    def mid_first():
        op("v", lambda: g.vector.memset(T.cw[:], 0.0), [], [A("cw", 0, 256)])

    def extra_first(k):
        if k == 1:
            act(A("cw", SS // 16, MA), A("pa", SS // 16, MA), ACT.Copy)
            act(A("cw", MA + SS // 16, 256), A("pa", MA + SS // 16, 256), ACT.Copy)
        if k == 2:
            cp(A("nq", 0, 512), A("nxi", 0, 512))
        if k == 3:
            cp(idh, idp)
            cp(capb, capf)

    doublings(mid_first, extra_first)
    values(0)

    sm = summed(0, 0)
    av = A("ps0", MA, 2 * MA)
    ts(av, sm, 0.0, None, ALU.is_gt)
    r_offsets(0, MA, av)
    rinit("s", 0, 1024)
    digits(0, MA, av, A("ps0", 0, MA), A("ps0", 2 * MA, 3 * MA))
    lists_mm(0, MA, "px0")
    act(A("yc", 0, 1024), A("y0", 0, 1024), ACT.Copy)
    rinit("v", 1024, 2048)
    lists_cp(0, MA, "px0")
    cp(A("yc", 1024, 2048), A("y0", 1024, 2048))
    sm = summed(0, 1)
    av = A("ps1", MA, 2 * MA)
    ts(av, sm, 0.0, None, ALU.is_gt)
    r_offsets(MA, 256, av)
    rinit("s", 2048, 3072)
    rinit("s", 3072, 3328)
    digits(MA, 256, av, A("ps1", 0, MA), A("ps1", 2 * MA, 3 * MA))
    w0_dma(1)
    lists_mm(MA, 256, "px1")
    rinit("v", 3328, S)
    ycopy(0, 2048, 3072)
    ycopy(0, 3072, S)
    doublings(lambda: lists_cp(MA, 256, "px1"), lambda k: None)
    values(1)

    g.sem_inc(T.sem["issued"], 1)
    total["issued"] = 1
    need("y", ("issued", 1))
    pieces = [("v", 0, 1024), ("s", 2560, 3328), ("v", 1024, 1792), ("v", 1792, 2560), ("s", 3328, S)]
    for q, lo, hi in pieces:
        if q == "v":
            ts(A("y0", lo, hi), A("y1", lo, hi), 0.0, capb, ALU.max, ALU.subtract)
            ts(A("m0", lo, hi), A("y0", lo, hi), -1.0, None, ALU.mult)
        else:
            act(A("y0", lo, hi), A("y1", lo, hi), ACT.Relu)
            act(A("m0", lo, hi), A("y0", lo, hi), ACT.Identity, bias=capf, scale=-1.0)
        dma("y", T.yr[:, lo:hi], T.m0[:, lo:hi], "s_yr", 16 * len(pieces), [A("m0", lo, hi)], [])
    for part in range(2):
        lo, hi = MA * part, MA * (part + 1)
        sm = summed(1, part)
        ts(A("yab", lo, hi), sm, 0.0, None, ALU.is_gt)
        dma("s", T.ya[:, lo:hi], T.yab[:, lo:hi], "s_ya", 32, [A("yab", lo, hi)], [])
    for sem in SEMAPHORES:
        if total.get(sem, 0) > waited.get(sem, 0):
            need("g", (sem, total[sem]))
